import numpy as np
import ml_dtypes


def mxq(x, axis, fmt="e4m3"):
    dtype, down = {"e4m3": (ml_dtypes.float8_e4m3fn, 7), "e5m2": (ml_dtypes.float8_e5m2, 14)}[fmt]
    v = np.moveaxis(np.asarray(x, np.float32).astype(ml_dtypes.bfloat16).astype(np.float64), axis, -1)
    blocks = v.reshape(v.shape[:-1] + (-1, 32))
    amax = np.abs(blocks).max(-1, keepdims=True)
    byte = np.maximum(np.where(amax > 0, np.frexp(amax)[1] - 1 + 127, 0) - down, 1)
    scale = np.exp2(byte - 127.0)
    codes = (blocks / scale).astype(np.float32).astype(dtype).astype(np.float64)
    return np.moveaxis((codes * scale).reshape(v.shape), -1, axis)


WIDE = False


def mx_kscale(k):
    if not WIDE:
        return np.ones(k)
    levels = np.array([30, -30])
    if k % 512:
        return np.exp2(np.random.permutation(np.resize(levels, k // 32))).repeat(32)
    a = np.empty((k // 512, 16))
    for p in range(k // 512):
        a[p, :8] = np.random.permutation(np.resize(levels, 8))
        for g in range(8):
            far = levels[np.abs(levels - a[p, g]) >= 10]
            a[p, g + 8] = far[np.random.randint(len(far))]
    return np.exp2(a.ravel()).repeat(32)


def f64(x):
    return np.asarray(x).astype(np.float64)


def striped(idx):
    return np.tile(np.asarray(idx).reshape(-1, 16).T, (8, 1)).astype(np.uint16)


def unstriped(offs):
    return offs[:16].T.reshape(-1).astype(np.int64)


E2M1 = np.array([0.0, 0.5, 1.0, 1.5, 2.0, 3.0, 4.0, 6.0, -0.0, -0.5, -1.0, -1.5, -2.0, -3.0, -4.0, -6.0])


def pack_weight(w, fmt):
    k, n = w.shape
    w = f64(np.asarray(w, np.float32).astype(ml_dtypes.bfloat16)).reshape(k // 32, 32, n)
    amax = np.abs(w).max(1)
    if fmt in ("e4m3", "e5m2"):
        byte = np.frexp(amax)[1] - 1 + 127 - (7 if fmt == "e4m3" else 14)
    else:
        mant, ex = np.frexp(amax / 6.0)
        byte = np.where(mant > 0.5, ex, ex - 1) + 127
    byte = np.clip(np.where(amax > 0, byte, 1), 1, 254)
    scaled = (w * np.exp2(127.0 - byte)[:, None, :]).reshape(k, n).astype(np.float32)
    by_word = np.ascontiguousarray(scaled.reshape(k // 512, 128, 4, n).transpose(0, 1, 3, 2))
    if fmt in ("e4m3", "e5m2"):
        words = by_word.astype(ml_dtypes.float8_e4m3fn if fmt == "e4m3" else ml_dtypes.float8_e5m2).view(np.uint8)
    else:
        c = by_word.astype(ml_dtypes.float4_e2m1fn).view(np.uint8) & 0xF
        words = (c[..., 0::2] | (c[..., 1::2] << 4)).reshape(k // 512, 128, 2 * n)
    return np.ascontiguousarray(words), np.ascontiguousarray(byte.astype(np.uint8).reshape(k // 512, 16, n))


def unpack_weight(words, scales, fmt):
    g, _, n = scales.shape
    words = np.ascontiguousarray(words).reshape(g, 128, n, -1)
    if fmt in ("e4m3", "e5m2"):
        vals = words.view(ml_dtypes.float8_e4m3fn if fmt == "e4m3" else ml_dtypes.float8_e5m2).astype(np.float64)
    else:
        nib = np.empty((g, 128, n, 4), np.uint8)
        nib[..., 0::2] = words & 0xF
        nib[..., 1::2] = words >> 4
        vals = E2M1[nib]
    vals = vals * np.repeat(np.exp2(scales.astype(np.float64) - 127.0), 8, axis=1)[..., None]
    return vals.transpose(0, 1, 3, 2).reshape(g * 512, n)


K, T, J, I, L, S, R, F, Z, N = 512, 512, 256, 128, 128, 512, 512, 512, 1024, 256


def setup_inputs():
    n = np.random.standard_normal
    idx = np.random.permutation(T)[:I]
    idx2 = np.random.permutation(S)[:L]
    idx3 = np.random.permutation(Z)[:J]
    fk = mx_kscale(K)
    fr = mx_kscale(R)
    ff = mx_kscale(F)
    wp = pack_weight(n((K, R)) * 1 / np.sqrt(K) * fk[:, None] * fr, "e2m1")
    w2p = pack_weight(n((F, R)) * 1 / np.sqrt(F) * ff[:, None] * fr, "e5m2")
    wbp = pack_weight(n((R, N)) * 1 / np.sqrt(R) / fr[:, None], "e5m2")
    return {
        "xa": (n((K, T)) / fk[:, None]).astype(np.float32),
        "xb": (n((K, S)) * 0.6 / fk[:, None]).astype(np.float32),
        "w_words": wp[0],
        "w_scales": wp[1],
        "xo": (n((F, Z))).astype(np.float32),
        "fl": (np.random.uniform(0.5, 2.0, (F, 1)) / ff[:, None]).astype(np.float32),
        "so": (n((F, J)) * 0.8).astype(np.float32),
        "w2_words": w2p[0],
        "w2_scales": w2p[1],
        "wb_words": wbp[0],
        "wb_scales": wbp[1],
        "rs": (1.0 * n((J, N))).astype(np.float32),
        "offs": striped(idx),
        "offs2": striped(idx2),
        "offs3": striped(idx3),
    }


def reference(xa, xb, w_words, w_scales, xo, fl, so, w2_words, w2_scales, wb_words, wb_scales, rs, offs, offs2, offs3):
    idx = unstriped(offs)
    idx2 = unstriped(offs2)
    idx3 = unstriped(offs3)
    wu = unpack_weight(w_words, w_scales, "e2m1")
    w2u = unpack_weight(w2_words, w2_scales, "e5m2")
    wbu = unpack_weight(wb_words, wb_scales, "e5m2")
    u = np.concatenate([f64(xa)[:, idx], f64(xb)[:, idx2]], axis=1)
    u2 = np.maximum(f64(xo)[:, idx3], f64(so)) * f64(fl)
    uq = mxq(u, 0, "e4m3")
    u2q = mxq(u2, 0, "e5m2")
    a = wu.T @ uq + w2u.T @ u2q
    hid = np.maximum(a, 0.0)
    hidq = mxq(hid, 0, "e5m2")
    p = hidq.T @ wbu
    pk2 = np.max(np.abs(p), axis=1, keepdims=True)
    y = p / (pk2 + 0.2) + 0.3 * f64(rs)
    return y

@@ -1,0 +1,211 @@
+from contextlib import ExitStack
+
+import concourse.mybir as mybir
+
+K, T, J, S, R, F, Z, N = 512, 512, 256, 512, 512, 512, 1024, 256
+FLOPS = 2 * J * (K * R + F * R + R * N)
+
+F32 = mybir.dt.float32
+BF16 = mybir.dt.bfloat16
+I32 = mybir.dt.int32
+U32 = mybir.dt.uint32
+U16 = mybir.dt.uint16
+U8 = mybir.dt.uint8
+E4M3 = mybir.dt.float8_e4m3fn_x4
+E5M2 = mybir.dt.float8_e5m2_x4
+E2M1 = mybir.dt.float4_e2m1fn_x4
+ALU = mybir.AluOpType
+ACT = mybir.ActivationFunctionType
+
+P = 128
+PACK = 4
+HALF = 128
+
+
+def tile_list_sum_joined_largest_plain_rowpeaks_kernel(
+    tc, xa, xb, w_words, w_scales, xo, fl, so, w2_words, w2_scales, wb_words, wb_scales, rs, offs, offs2, offs3, out
+):
+    nc = tc.nc
+    with ExitStack() as ctx:
+        sb = ctx.enter_context(tc.tile_pool(name="sb", bufs=1))
+        ps = ctx.enter_context(tc.psum_pool(name="ps", bufs=1))
+
+        def load_scale_rows(queue, tile, scales, quadrants):
+            rows = scales[0].bitcast(I32)
+            for q in quadrants:
+                queue.dma_start(out=tile[32 * q : 32 * q + 4, :].bitcast(I32), in_=rows[4 * q : 4 * q + 4, :])
+
+        w2_scale_raw = sb.tile([P, R], U8)
+        w_scale_raw = sb.tile([P, R], U8)
+        wb_scale = sb.tile([P, N], U8, align_bytes=64)
+        fl_sb = sb.tile([P, PACK], F32)
+        for tile in (w2_scale_raw, w_scale_raw, wb_scale):
+            nc.gpsimd.memset(tile[:].bitcast(I32), 0)
+        nc.gpsimd.dma_start(out=fl_sb[:], in_=fl.rearrange("(p t) o -> p (t o)", t=PACK))
+        load_scale_rows(nc.gpsimd, wb_scale, wb_scales, range(4))
+
+        xo_rows = xo.rearrange("(p t) z -> p t z", t=PACK)
+        so_sb = sb.tile([P, PACK, J], F32)
+        xo_sb = [sb.tile([P, Z], F32, name="xo%d" % t) for t in range(PACK)]
+        list_o = sb.tile([P, J // 16], U16)
+        lists = [sb.tile([P, HALF // 16], U16, name="list_a"), sb.tile([P, HALF // 16], U16, name="list_b")]
+        w2_raw = sb.tile([P, R], U32)
+        w_raw = sb.tile([P, 2 * R], U8)
+        wb_sb = sb.tile([P, N], U32, align_bytes=64)
+        xa01 = sb.tile([P, 2 * T], F32)
+        planes = [
+            [xa01[:, 0:T], xa01[:, T : 2 * T]] + [sb.tile([P, T], F32, name="xa%d" % t)[:] for t in (2, 3)],
+            [sb.tile([P, S], F32, name="xb%d" % t)[:] for t in range(PACK)],
+        ]
+        rs_sb = [sb.tile([P, N], F32, name="rs%d" % h) for h in range(2)]
+        x_rows = [xa.rearrange("(p t) c -> p t c", t=PACK), xb.rearrange("(p t) c -> p t c", t=PACK)]
+
+        def load_plane(h, t):
+            nc.sync.dma_start(out=planes[h][t], in_=x_rows[h][:, t, :])
+
+        nc.sync.dma_start(out=xo_sb[0][:], in_=xo_rows[:, 0, :])
+        nc.sync.dma_start(list_o[:], offs3)
+        load_scale_rows(nc.sync, w2_scale_raw, w2_scales, range(4))
+        nc.sync.dma_start(out=so_sb[:], in_=so.rearrange("(p t) j -> p t j", t=PACK))
+        nc.sync.dma_start(out=xo_sb[1][:], in_=xo_rows[:, 1, :])
+        load_scale_rows(nc.sync, w_scale_raw, w_scales, range(4))
+        nc.sync.dma_start(out=xo_sb[2][:], in_=xo_rows[:, 2, :])
+        nc.sync.dma_start(out=xo_sb[3][:], in_=xo_rows[:, 3, :])
+        nc.sync.dma_start(lists[0][:], offs)
+        nc.sync.dma_start(out=w2_raw[:].bitcast(I32), in_=w2_words[0].rearrange("p n t -> p (n t)").bitcast(I32))
+        nc.sync.dma_start(out=xa01[:], in_=xa.rearrange("(p t) c -> p (t c)", t=PACK)[:, 0 : 2 * T])
+        load_plane(0, 2)
+        load_plane(0, 3)
+        nc.sync.dma_start(out=w_raw[:].bitcast(I32), in_=w_words[0].bitcast(I32))
+        nc.sync.dma_start(lists[1][:], offs2)
+        for t in range(PACK):
+            load_plane(1, t)
+        nc.sync.dma_start(out=wb_sb[:].bitcast(I32), in_=wb_words[0].rearrange("p n t -> p (n t)").bitcast(I32))
+        for h in range(2):
+            nc.sync.dma_start(out=rs_sb[h][:], in_=rs[h * HALF : (h + 1) * HALF, :])
+
+        def deal_columns(copy, dealt, raw):
+            copy(out=dealt.rearrange("p (t m) -> p m t", t=PACK), in_=raw.rearrange("p (m t) -> p m t", t=PACK))
+
+        w2_scale = sb.tile([P, R], U8, align_bytes=64)
+        w_scale = sb.tile([P, R], U8, align_bytes=64)
+        deal_columns(nc.vector.tensor_copy, w2_scale[:], w2_scale_raw[:])
+        u2_bf = sb.tile([P, J, PACK], BF16, align_bytes=64)
+        picked = [sb.tile([P, J], F32, name="picked%d" % t) for t in range(PACK)]
+        larger = [sb.tile([P, J], F32, name="larger%d" % t) for t in range(PACK)]
+
+        def side_gather(t, j0, j1):
+            nc.scalar.activation(picked[t][:, j0:j1], xo_sb[t][:].indirect(list_o[:, j0 // 16 : j1 // 16]), ACT.Copy)
+
+        def side_larger(t, j0, j1):
+            nc.vector.tensor_tensor(larger[t][:, j0:j1], picked[t][:, j0:j1], so_sb[:, t, j0:j1], ALU.max)
+
+        def side_scale(t, j0, j1):
+            nc.vector.tensor_scalar(u2_bf[:, j0:j1, t], larger[t][:, j0:j1], fl_sb[:, t : t + 1], None, ALU.mult)
+
+        for t in range(PACK - 1):
+            side_gather(t, 0, J)
+            side_larger(t, 0, J)
+            if t == 0:
+                deal_columns(nc.vector.tensor_copy, w_scale[:], w_scale_raw[:])
+            side_scale(t, 0, J)
+        for step in (side_gather, side_larger, side_scale):
+            for h in range(2):
+                step(PACK - 1, h * HALF, (h + 1) * HALF)
+        w2_dealt = sb.tile([P, R], U32, align_bytes=64)
+        deal_columns(nc.scalar.copy, w2_dealt[:], w2_raw[:])
+        hid_ps = [ps.tile([P, PACK, HALF], F32, name="hid_ps%d" % h) for h in range(2)]
+        for h in range(2):
+            u2_codes = sb.tile([P, HALF], U32, name="u2_codes%d" % h, align_bytes=64)
+            u2_scale = sb.tile([P, HALF], U8, name="u2_scale%d" % h, align_bytes=64)
+            nc.vector.quantize_mx(
+                out=u2_codes[:].bitcast(E5M2),
+                scales=u2_scale[:],
+                in_=u2_bf[:, h * HALF : (h + 1) * HALF, :].rearrange("p j t -> p (j t)"),
+            )
+            for t in range(PACK):
+                nc.tensor.matmul_mx(
+                    out=hid_ps[h][:, t, :],
+                    lhsT=w2_dealt[:, t * P : (t + 1) * P].bitcast(E5M2),
+                    lhsT_scale=w2_scale[:, t * P : (t + 1) * P],
+                    rhs=u2_codes[:].bitcast(E5M2),
+                    rhs_scale=u2_scale[:],
+                    start=(t == 0),
+                    stop=False,
+                )
+        w_dealt = sb.tile([P, 2 * R], U8, align_bytes=64)
+        deal_columns(nc.scalar.copy, w_dealt[:].bitcast(U16), w_raw[:].bitcast(U16))
+
+        u_bf = [sb.tile([P, HALF, PACK], BF16, name="u_bf%d" % h, align_bytes=64) for h in range(2)]
+        hid_bf = [sb.tile([P, HALF, PACK], BF16, name="hid_bf%d" % h, align_bytes=64) for h in range(2)]
+        p_ps = [ps.tile([P, N], F32, name="p_ps%d" % h) for h in range(2)]
+
+        def gather(h, t):
+            nc.vector.tensor_copy(u_bf[h][:, :, t], planes[h][t].indirect(lists[h][:]))
+
+        def first_layer(h):
+            u_codes = sb.tile([P, HALF], U32, name="u_codes%d" % h, align_bytes=64)
+            u_scale = sb.tile([P, HALF], U8, name="u_scale%d" % h, align_bytes=64)
+            nc.vector.quantize_mx(
+                out=u_codes[:].bitcast(E4M3), scales=u_scale[:], in_=u_bf[h][:].rearrange("p j t -> p (j t)")
+            )
+            for t in range(PACK):
+                nc.tensor.matmul_mx(
+                    out=hid_ps[h][:, t, :],
+                    lhsT=w_dealt[:, 2 * t * P : 2 * (t + 1) * P].bitcast(E2M1),
+                    lhsT_scale=w_scale[:, t * P : (t + 1) * P],
+                    rhs=u_codes[:].bitcast(E4M3),
+                    rhs_scale=u_scale[:],
+                    start=False,
+                    stop=(t == PACK - 1),
+                )
+            nc.scalar.activation(hid_bf[h][:], hid_ps[h][:].rearrange("p t j -> p j t"), ACT.Relu)
+
+        def second_layer(h):
+            hid_codes = sb.tile([P, HALF], U32, name="hid_codes%d" % h, align_bytes=64)
+            hid_scale = sb.tile([P, HALF], U8, name="hid_scale%d" % h, align_bytes=64)
+            nc.vector.quantize_mx(
+                out=hid_codes[:].bitcast(E5M2), scales=hid_scale[:], in_=hid_bf[h][:].rearrange("p j t -> p (j t)")
+            )
+            nc.tensor.matmul_mx(
+                out=p_ps[h][:],
+                lhsT=hid_codes[:].bitcast(E5M2),
+                lhsT_scale=hid_scale[:],
+                rhs=wb_sb[:].bitcast(E5M2),
+                rhs_scale=wb_scale[:],
+                start=True,
+                stop=True,
+            )
+
+        inverse = [sb.tile([P, 1], F32, name="inverse%d" % h) for h in range(2)]
+        residual = [sb.tile([P, N], F32, name="residual%d" % h) for h in range(2)]
+
+        def row_peaks(h):
+            size = sb.tile([P, N], F32, name="size%d" % h)
+            divisor = sb.tile([P, 1], F32, name="divisor%d" % h)
+            nc.scalar.activation(size[:], p_ps[h][:], ACT.Abs)
+            nc.vector.tensor_scalar(size[:], size[:], 0.2, None, ALU.add, ALU.max, accum_out=divisor[:])
+            nc.vector.reciprocal(inverse[h][:], divisor[:])
+
+        def scale_residual(h):
+            nc.vector.tensor_scalar(residual[h][:], rs_sb[h][:], 0.3, None, ALU.mult)
+
+        def finish(h):
+            result = sb.tile([P, N], F32, name="result%d" % h)
+            nc.vector.scalar_tensor_tensor(result[:], p_ps[h][:], inverse[h][:], residual[h][:], ALU.mult, ALU.add)
+            nc.sync.dma_start(out=out[h * HALF : (h + 1) * HALF, :], in_=result[:])
+
+        for t in range(PACK):
+            gather(0, t)
+        first_layer(0)
+        for t in range(PACK):
+            gather(1, t)
+        second_layer(0)
+        first_layer(1)
+        row_peaks(0)
+        scale_residual(0)
+        second_layer(1)
+        finish(0)
+        scale_residual(1)
+        row_peaks(1)
+        finish(1)

@@ -30,19 +30,17 @@ def tile_list_sum_joined_largest_plain_rowpeaks_kernel(
         sb = ctx.enter_context(tc.tile_pool(name="sb", bufs=1))
         ps = ctx.enter_context(tc.psum_pool(name="ps", bufs=1))
 
-        def load_scale_rows(queue, tile, scales, quadrants):
+        def load_scale_rows(tile, scales, quadrants):
             rows = scales[0].bitcast(I32)
             for q in quadrants:
-                queue.dma_start(out=tile[32 * q : 32 * q + 4, :].bitcast(I32), in_=rows[4 * q : 4 * q + 4, :])
+                nc.sync.dma_start(out=tile[32 * q : 32 * q + 4, :].bitcast(I32), in_=rows[4 * q : 4 * q + 4, :])
 
         w2_scale_raw = sb.tile([P, R], U8)
         w_scale_raw = sb.tile([P, R], U8)
         wb_scale = sb.tile([P, N], U8, align_bytes=64)
         fl_sb = sb.tile([P, PACK], F32)
         for tile in (w2_scale_raw, w_scale_raw, wb_scale):
-            nc.gpsimd.memset(tile[:].bitcast(I32), 0)
-        nc.gpsimd.dma_start(out=fl_sb[:], in_=fl.rearrange("(p t) o -> p (t o)", t=PACK))
-        load_scale_rows(nc.gpsimd, wb_scale, wb_scales, range(4))
+            nc.vector.memset(tile[:].bitcast(I32), 0)
 
         xo_rows = xo.rearrange("(p t) z -> p t z", t=PACK)
         so_sb = sb.tile([P, PACK, J], F32)
@@ -52,44 +50,50 @@ def tile_list_sum_joined_largest_plain_rowpeaks_kernel(
         w2_raw = sb.tile([P, R], U32)
         w_raw = sb.tile([P, 2 * R], U8)
         wb_sb = sb.tile([P, N], U32, align_bytes=64)
-        xa01 = sb.tile([P, 2 * T], F32)
+        pairs = [sb.tile([P, 2 * T], F32, name="x01_%d" % h) for h in range(2)]
         planes = [
-            [xa01[:, 0:T], xa01[:, T : 2 * T]] + [sb.tile([P, T], F32, name="xa%d" % t)[:] for t in (2, 3)],
-            [sb.tile([P, S], F32, name="xb%d" % t)[:] for t in range(PACK)],
+            [pairs[h][:, 0:T], pairs[h][:, T : 2 * T]] + [sb.tile([P, T], F32, name="x%d_%d" % (t, h))[:] for t in (2, 3)]
+            for h in range(2)
         ]
-        rs_sb = [sb.tile([P, N], F32, name="rs%d" % h) for h in range(2)]
-        x_rows = [xa.rearrange("(p t) c -> p t c", t=PACK), xb.rearrange("(p t) c -> p t c", t=PACK)]
+        rs_sb = sb.tile([P, 2, N], F32)
+        x_rows = [xa.rearrange("(p t) c -> p (t c)", t=PACK), xb.rearrange("(p t) c -> p (t c)", t=PACK)]
 
         def load_plane(h, t):
-            nc.sync.dma_start(out=planes[h][t], in_=x_rows[h][:, t, :])
+            nc.sync.dma_start(out=planes[h][t], in_=x_rows[h][:, t * T : (t + 1) * T])
+
+        def load_pair(h):
+            nc.sync.dma_start(out=pairs[h][:], in_=x_rows[h][:, 0 : 2 * T])
 
         nc.sync.dma_start(out=xo_sb[0][:], in_=xo_rows[:, 0, :])
         nc.sync.dma_start(list_o[:], offs3)
-        load_scale_rows(nc.sync, w2_scale_raw, w2_scales, range(4))
         nc.sync.dma_start(out=so_sb[:], in_=so.rearrange("(p t) j -> p t j", t=PACK))
+        nc.sync.dma_start(out=fl_sb[:], in_=fl.rearrange("(p t) o -> p (t o)", t=PACK))
         nc.sync.dma_start(out=xo_sb[1][:], in_=xo_rows[:, 1, :])
-        load_scale_rows(nc.sync, w_scale_raw, w_scales, range(4))
+        load_scale_rows(w2_scale_raw, w2_scales, range(0, 3))
         nc.sync.dma_start(out=xo_sb[2][:], in_=xo_rows[:, 2, :])
+        load_scale_rows(w2_scale_raw, w2_scales, range(3, 4))
         nc.sync.dma_start(out=xo_sb[3][:], in_=xo_rows[:, 3, :])
-        nc.sync.dma_start(lists[0][:], offs)
+        load_scale_rows(w_scale_raw, w_scales, range(0, 2))
         nc.sync.dma_start(out=w2_raw[:].bitcast(I32), in_=w2_words[0].rearrange("p n t -> p (n t)").bitcast(I32))
-        nc.sync.dma_start(out=xa01[:], in_=xa.rearrange("(p t) c -> p (t c)", t=PACK)[:, 0 : 2 * T])
+        nc.sync.dma_start(lists[0][:], offs)
+        load_pair(0)
+        load_scale_rows(w_scale_raw, w_scales, range(2, 4))
         load_plane(0, 2)
-        load_plane(0, 3)
         nc.sync.dma_start(out=w_raw[:].bitcast(I32), in_=w_words[0].bitcast(I32))
+        load_plane(0, 3)
         nc.sync.dma_start(lists[1][:], offs2)
-        for t in range(PACK):
-            load_plane(1, t)
+        load_pair(1)
+        load_plane(1, 2)
+        load_plane(1, 3)
+        load_scale_rows(wb_scale, wb_scales, range(4))
         nc.sync.dma_start(out=wb_sb[:].bitcast(I32), in_=wb_words[0].rearrange("p n t -> p (n t)").bitcast(I32))
-        for h in range(2):
-            nc.sync.dma_start(out=rs_sb[h][:], in_=rs[h * HALF : (h + 1) * HALF, :])
+        nc.sync.dma_start(out=rs_sb[:], in_=rs.rearrange("(h p) n -> p h n", h=2))
 
         def deal_columns(copy, dealt, raw):
             copy(out=dealt.rearrange("p (t m) -> p m t", t=PACK), in_=raw.rearrange("p (m t) -> p m t", t=PACK))
 
         w2_scale = sb.tile([P, R], U8, align_bytes=64)
         w_scale = sb.tile([P, R], U8, align_bytes=64)
-        deal_columns(nc.vector.tensor_copy, w2_scale[:], w2_scale_raw[:])
         u2_bf = sb.tile([P, J, PACK], BF16, align_bytes=64)
         picked = [sb.tile([P, J], F32, name="picked%d" % t) for t in range(PACK)]
         larger = [sb.tile([P, J], F32, name="larger%d" % t) for t in range(PACK)]
@@ -106,8 +110,8 @@ def tile_list_sum_joined_largest_plain_rowpeaks_kernel(
         for t in range(PACK - 1):
             side_gather(t, 0, J)
             side_larger(t, 0, J)
-            if t == 0:
-                deal_columns(nc.vector.tensor_copy, w_scale[:], w_scale_raw[:])
+            if t == PACK - 2:
+                deal_columns(nc.vector.tensor_copy, w2_scale[:], w2_scale_raw[:])
             side_scale(t, 0, J)
         for step in (side_gather, side_larger, side_scale):
             for h in range(2):
@@ -162,7 +166,7 @@ def tile_list_sum_joined_largest_plain_rowpeaks_kernel(
             nc.scalar.activation(hid_bf[h][:], hid_ps[h][:].rearrange("p t j -> p j t"), ACT.Relu)
 
         def second_layer(h):
-            hid_codes = sb.tile([P, HALF], U32, name="hid_codes%d" % h, align_bytes=64)
+            hid_codes = sb.tile([P, HALF], U32, name="hid_codes%d" % h, tag="u_bf%d" % (1 - h), align_bytes=64)
             hid_scale = sb.tile([P, HALF], U8, name="hid_scale%d" % h, align_bytes=64)
             nc.vector.quantize_mx(
                 out=hid_codes[:].bitcast(E5M2), scales=hid_scale[:], in_=hid_bf[h][:].rearrange("p j t -> p (j t)")
@@ -178,7 +182,7 @@ def tile_list_sum_joined_largest_plain_rowpeaks_kernel(
             )
 
         inverse = [sb.tile([P, 1], F32, name="inverse%d" % h) for h in range(2)]
-        residual = [sb.tile([P, N], F32, name="residual%d" % h) for h in range(2)]
+        residual = sb.tile([P, 2, N], F32)
 
         def row_peaks(h):
             size = sb.tile([P, N], F32, name="size%d" % h)
@@ -187,25 +191,23 @@ def tile_list_sum_joined_largest_plain_rowpeaks_kernel(
             nc.vector.tensor_scalar(size[:], size[:], 0.2, None, ALU.add, ALU.max, accum_out=divisor[:])
             nc.vector.reciprocal(inverse[h][:], divisor[:])
 
-        def scale_residual(h):
-            nc.vector.tensor_scalar(residual[h][:], rs_sb[h][:], 0.3, None, ALU.mult)
-
         def finish(h):
             result = sb.tile([P, N], F32, name="result%d" % h)
-            nc.vector.scalar_tensor_tensor(result[:], p_ps[h][:], inverse[h][:], residual[h][:], ALU.mult, ALU.add)
+            nc.vector.scalar_tensor_tensor(result[:], p_ps[h][:], inverse[h][:], residual[:, h, :], ALU.mult, ALU.add)
             nc.sync.dma_start(out=out[h * HALF : (h + 1) * HALF, :], in_=result[:])
 
-        for t in range(PACK):
+        for t in range(PACK - 1):
             gather(0, t)
+        deal_columns(nc.vector.tensor_copy, w_scale[:], w_scale_raw[:])
+        gather(0, PACK - 1)
         first_layer(0)
         for t in range(PACK):
             gather(1, t)
-        second_layer(0)
         first_layer(1)
-        row_peaks(0)
-        scale_residual(0)
+        second_layer(0)
+        nc.vector.tensor_scalar(residual[:], rs_sb[:], 0.3, None, ALU.mult)
         second_layer(1)
+        row_peaks(0)
         finish(0)
-        scale_residual(1)
         row_peaks(1)
         finish(1)

@@ -50,19 +50,16 @@ def tile_list_sum_joined_largest_plain_rowpeaks_kernel(
         w2_raw = sb.tile([P, R], U32)
         w_raw = sb.tile([P, 2 * R], U8)
         wb_sb = sb.tile([P, N], U32, align_bytes=64)
-        pairs = [sb.tile([P, 2 * T], F32, name="x01_%d" % h) for h in range(2)]
+        xa_pair = sb.tile([P, 2 * T], F32)
         planes = [
-            [pairs[h][:, 0:T], pairs[h][:, T : 2 * T]] + [sb.tile([P, T], F32, name="x%d_%d" % (t, h))[:] for t in (2, 3)]
-            for h in range(2)
+            [xa_pair[:, 0:T], xa_pair[:, T : 2 * T]] + [sb.tile([P, T], F32, name="xa%d" % t)[:] for t in (2, 3)],
+            [sb.tile([P, S], F32, name="xb%d" % t)[:] for t in range(PACK)],
         ]
         rs_sb = sb.tile([P, 2, N], F32)
         x_rows = [xa.rearrange("(p t) c -> p (t c)", t=PACK), xb.rearrange("(p t) c -> p (t c)", t=PACK)]
 
         def load_plane(h, t):
             nc.sync.dma_start(out=planes[h][t], in_=x_rows[h][:, t * T : (t + 1) * T])
-
-        def load_pair(h):
-            nc.sync.dma_start(out=pairs[h][:], in_=x_rows[h][:, 0 : 2 * T])
 
         nc.sync.dma_start(out=xo_sb[0][:], in_=xo_rows[:, 0, :])
         nc.sync.dma_start(list_o[:], offs3)
@@ -76,15 +73,14 @@ def tile_list_sum_joined_largest_plain_rowpeaks_kernel(
         load_scale_rows(w_scale_raw, w_scales, range(0, 2))
         nc.sync.dma_start(out=w2_raw[:].bitcast(I32), in_=w2_words[0].rearrange("p n t -> p (n t)").bitcast(I32))
         nc.sync.dma_start(lists[0][:], offs)
-        load_pair(0)
+        nc.sync.dma_start(out=xa_pair[:], in_=x_rows[0][:, 0 : 2 * T])
         load_scale_rows(w_scale_raw, w_scales, range(2, 4))
         load_plane(0, 2)
         nc.sync.dma_start(out=w_raw[:].bitcast(I32), in_=w_words[0].bitcast(I32))
         load_plane(0, 3)
         nc.sync.dma_start(lists[1][:], offs2)
-        load_pair(1)
-        load_plane(1, 2)
-        load_plane(1, 3)
+        for t in range(PACK):
+            load_plane(1, t)
         load_scale_rows(wb_scale, wb_scales, range(4))
         nc.sync.dma_start(out=wb_sb[:].bitcast(I32), in_=wb_words[0].rearrange("p n t -> p (n t)").bitcast(I32))
         nc.sync.dma_start(out=rs_sb[:], in_=rs.rearrange("(h p) n -> p h n", h=2))
@@ -92,11 +88,9 @@ def tile_list_sum_joined_largest_plain_rowpeaks_kernel(
         def deal_columns(copy, dealt, raw):
             copy(out=dealt.rearrange("p (t m) -> p m t", t=PACK), in_=raw.rearrange("p (m t) -> p m t", t=PACK))
 
-        w2_scale = sb.tile([P, R], U8, align_bytes=64)
-        w_scale = sb.tile([P, R], U8, align_bytes=64)
         u2_bf = sb.tile([P, J, PACK], BF16, align_bytes=64)
         picked = [sb.tile([P, J], F32, name="picked%d" % t) for t in range(PACK)]
-        larger = [sb.tile([P, J], F32, name="larger%d" % t) for t in range(PACK)]
+        larger = [sb.tile([P, J], F32, name="larger%d" % t, align_bytes=64) for t in range(PACK)]
 
         def side_gather(t, j0, j1):
             nc.scalar.activation(picked[t][:, j0:j1], xo_sb[t][:].indirect(list_o[:, j0 // 16 : j1 // 16]), ACT.Copy)
@@ -111,6 +105,7 @@ def tile_list_sum_joined_largest_plain_rowpeaks_kernel(
             side_gather(t, 0, J)
             side_larger(t, 0, J)
             if t == PACK - 2:
+                w2_scale = sb.tile([P, R], U8, tag="larger1", align_bytes=64)
                 deal_columns(nc.vector.tensor_copy, w2_scale[:], w2_scale_raw[:])
             side_scale(t, 0, J)
         for step in (side_gather, side_larger, side_scale):
@@ -118,55 +113,51 @@ def tile_list_sum_joined_largest_plain_rowpeaks_kernel(
                 step(PACK - 1, h * HALF, (h + 1) * HALF)
         w2_dealt = sb.tile([P, R], U32, align_bytes=64)
         deal_columns(nc.scalar.copy, w2_dealt[:], w2_raw[:])
-        hid_ps = [ps.tile([P, PACK, HALF], F32, name="hid_ps%d" % h) for h in range(2)]
-        for h in range(2):
-            u2_codes = sb.tile([P, HALF], U32, name="u2_codes%d" % h, align_bytes=64)
-            u2_scale = sb.tile([P, HALF], U8, name="u2_scale%d" % h, align_bytes=64)
-            nc.vector.quantize_mx(
-                out=u2_codes[:].bitcast(E5M2),
-                scales=u2_scale[:],
-                in_=u2_bf[:, h * HALF : (h + 1) * HALF, :].rearrange("p j t -> p (j t)"),
-            )
-            for t in range(PACK):
-                nc.tensor.matmul_mx(
-                    out=hid_ps[h][:, t, :],
-                    lhsT=w2_dealt[:, t * P : (t + 1) * P].bitcast(E5M2),
-                    lhsT_scale=w2_scale[:, t * P : (t + 1) * P],
-                    rhs=u2_codes[:].bitcast(E5M2),
-                    rhs_scale=u2_scale[:],
-                    start=(t == 0),
-                    stop=False,
-                )
         w_dealt = sb.tile([P, 2 * R], U8, align_bytes=64)
-        deal_columns(nc.scalar.copy, w_dealt[:].bitcast(U16), w_raw[:].bitcast(U16))
 
         u_bf = [sb.tile([P, HALF, PACK], BF16, name="u_bf%d" % h, align_bytes=64) for h in range(2)]
-        hid_bf = [sb.tile([P, HALF, PACK], BF16, name="hid_bf%d" % h, align_bytes=64) for h in range(2)]
+        hid_bf = []
         p_ps = [ps.tile([P, N], F32, name="p_ps%d" % h) for h in range(2)]
+
+        hid_ps = [ps.tile([P, PACK, HALF], F32, name="hid_ps%d" % h) for h in range(2)]
+
+        def gather_pair(h):
+            pair = sb.tile([P, 2, HALF], F32, name="pair%d" % h, align_bytes=64)
+            for t in range(2):
+                nc.scalar.activation(pair[:, t, :], planes[h][t].indirect(lists[h][:]), ACT.Copy)
+            gather(h, 2)
+            nc.vector.tensor_copy(u_bf[h][:, :, 0:2], pair[:].rearrange("p t j -> p j t"))
 
         def gather(h, t):
             nc.vector.tensor_copy(u_bf[h][:, :, t], planes[h][t].indirect(lists[h][:]))
 
-        def first_layer(h):
-            u_codes = sb.tile([P, HALF], U32, name="u_codes%d" % h, align_bytes=64)
-            u_scale = sb.tile([P, HALF], U8, name="u_scale%d" % h, align_bytes=64)
-            nc.vector.quantize_mx(
-                out=u_codes[:].bitcast(E4M3), scales=u_scale[:], in_=u_bf[h][:].rearrange("p j t -> p (j t)")
-            )
+        def quantise(values, fmt, name, tag):
+            codes = sb.tile([P, HALF], U32, name=name + "_codes", tag=tag, align_bytes=64)
+            scale = sb.tile([P, HALF], U8, name=name + "_scale", align_bytes=64)
+            nc.vector.quantize_mx(out=codes[:].bitcast(fmt), scales=scale[:], in_=values.rearrange("p j t -> p (j t)"))
+            return codes[:].bitcast(fmt), scale[:]
+
+        def first_layer_passes(h, weights, weight_scale, moving, opens):
             for t in range(PACK):
                 nc.tensor.matmul_mx(
                     out=hid_ps[h][:, t, :],
-                    lhsT=w_dealt[:, 2 * t * P : 2 * (t + 1) * P].bitcast(E2M1),
-                    lhsT_scale=w_scale[:, t * P : (t + 1) * P],
-                    rhs=u_codes[:].bitcast(E4M3),
-                    rhs_scale=u_scale[:],
-                    start=False,
-                    stop=(t == PACK - 1),
+                    lhsT=weights[t],
+                    lhsT_scale=weight_scale[:, t * P : (t + 1) * P],
+                    rhs=moving[0],
+                    rhs_scale=moving[1],
+                    start=(opens and t == 0),
+                    stop=(not opens and t == PACK - 1),
                 )
+
+        w_slices = [w_dealt[:, 2 * t * P : 2 * (t + 1) * P].bitcast(E2M1) for t in range(PACK)]
+        w2_slices = [w2_dealt[:, t * P : (t + 1) * P].bitcast(E5M2) for t in range(PACK)]
+
+        def relu(h):
+            hid_bf.append(sb.tile([P, HALF, PACK], BF16, name="hid_bf%d" % h, align_bytes=64))
             nc.scalar.activation(hid_bf[h][:], hid_ps[h][:].rearrange("p t j -> p j t"), ACT.Relu)
 
         def second_layer(h):
-            hid_codes = sb.tile([P, HALF], U32, name="hid_codes%d" % h, tag="u_bf%d" % (1 - h), align_bytes=64)
+            hid_codes = sb.tile([P, HALF], U32, name="hid_codes%d" % h, tag="u_bf1" if h == 0 else "hid_codes1", align_bytes=64)
             hid_scale = sb.tile([P, HALF], U8, name="hid_scale%d" % h, align_bytes=64)
             nc.vector.quantize_mx(
                 out=hid_codes[:].bitcast(E5M2), scales=hid_scale[:], in_=hid_bf[h][:].rearrange("p j t -> p (j t)")
@@ -196,14 +187,23 @@ def tile_list_sum_joined_largest_plain_rowpeaks_kernel(
             nc.vector.scalar_tensor_tensor(result[:], p_ps[h][:], inverse[h][:], residual[:, h, :], ALU.mult, ALU.add)
             nc.sync.dma_start(out=out[h * HALF : (h + 1) * HALF, :], in_=result[:])
 
-        for t in range(PACK - 1):
-            gather(0, t)
+        w_scale = sb.tile([P, R], U8, tag="larger3", align_bytes=64)
         deal_columns(nc.vector.tensor_copy, w_scale[:], w_scale_raw[:])
-        gather(0, PACK - 1)
-        first_layer(0)
+        gather_pair(0)
+        deal_columns(nc.scalar.copy, w_dealt[:].bitcast(U16), w_raw[:].bitcast(U16))
+        u2_first = quantise(u2_bf[:, 0:HALF, :], E5M2, "u2_first", "u2_first_codes")
+        first_layer_passes(0, w2_slices, w2_scale, u2_first, True)
+        gather(0, 3)
+        u_first = quantise(u_bf[0][:], E4M3, "u_first", "u_first_codes")
+        first_layer_passes(0, w_slices, w_scale, u_first, False)
+        u2_second = quantise(u2_bf[:, HALF:J, :], E5M2, "u2_second", "u2_second_codes")
+        first_layer_passes(1, w2_slices, w2_scale, u2_second, True)
         for t in range(PACK):
             gather(1, t)
-        first_layer(1)
+        relu(0)
+        u_second = quantise(u_bf[1][:], E4M3, "u_second", "u_second_codes")
+        first_layer_passes(1, w_slices, w_scale, u_second, False)
+        relu(1)
         second_layer(0)
         nc.vector.tensor_scalar(residual[:], rs_sb[:], 0.3, None, ALU.mult)
         second_layer(1)

@@ -30,29 +30,32 @@ def tile_list_sum_joined_largest_plain_rowpeaks_kernel(
         sb = ctx.enter_context(tc.tile_pool(name="sb", bufs=1))
         ps = ctx.enter_context(tc.psum_pool(name="ps", bufs=1))
 
-        def load_scale_rows(tile, scales, quadrants):
+        def load_scale_rows(queue, tile, scales, quadrants):
             rows = scales[0].bitcast(I32)
             for q in quadrants:
-                nc.sync.dma_start(out=tile[32 * q : 32 * q + 4, :].bitcast(I32), in_=rows[4 * q : 4 * q + 4, :])
+                queue.dma_start(out=tile[32 * q : 32 * q + 4, :].bitcast(I32), in_=rows[4 * q : 4 * q + 4, :])
 
         w2_scale_raw = sb.tile([P, R], U8)
         w_scale_raw = sb.tile([P, R], U8)
         wb_scale = sb.tile([P, N], U8, align_bytes=64)
         fl_sb = sb.tile([P, PACK], F32)
-        for tile in (w2_scale_raw, w_scale_raw, wb_scale):
-            nc.vector.memset(tile[:].bitcast(I32), 0)
+        nc.vector.memset(w2_scale_raw[:].bitcast(I32), 0)
+        for tile, scales in ((w_scale_raw, w_scales), (wb_scale, wb_scales)):
+            nc.gpsimd.memset(tile[:].bitcast(I32), 0)
+            load_scale_rows(nc.gpsimd, tile, scales, range(4))
 
-        xo_rows = xo.rearrange("(p t) z -> p t z", t=PACK)
+        xo_rows = xo.rearrange("(p t) z -> p (t z)", t=PACK)
         so_sb = sb.tile([P, PACK, J], F32)
-        xo_sb = [sb.tile([P, Z], F32, name="xo%d" % t) for t in range(PACK)]
+        xo_planes = [sb.tile([P, Z], F32, name="xo%d" % t)[:] for t in range(PACK)]
         list_o = sb.tile([P, J // 16], U16)
         lists = [sb.tile([P, HALF // 16], U16, name="list_a"), sb.tile([P, HALF // 16], U16, name="list_b")]
         w2_raw = sb.tile([P, R], U32)
         w_raw = sb.tile([P, 2 * R], U8)
         wb_sb = sb.tile([P, N], U32, align_bytes=64)
-        xa_pair = sb.tile([P, 2 * T], F32)
+        xa_first = sb.tile([P, 3 * T], F32)
+        xa_last = sb.tile([P, T], F32)
         planes = [
-            [xa_pair[:, 0:T], xa_pair[:, T : 2 * T]] + [sb.tile([P, T], F32, name="xa%d" % t)[:] for t in (2, 3)],
+            [xa_first[:, t * T : (t + 1) * T] for t in range(3)] + [xa_last[:]],
             [sb.tile([P, S], F32, name="xb%d" % t)[:] for t in range(PACK)],
         ]
         rs_sb = sb.tile([P, 2, N], F32)
@@ -61,27 +64,24 @@ def tile_list_sum_joined_largest_plain_rowpeaks_kernel(
         def load_plane(h, t):
             nc.sync.dma_start(out=planes[h][t], in_=x_rows[h][:, t * T : (t + 1) * T])
 
-        nc.sync.dma_start(out=xo_sb[0][:], in_=xo_rows[:, 0, :])
+        nc.sync.dma_start(out=xo_planes[0], in_=xo_rows[:, 0:Z])
         nc.sync.dma_start(list_o[:], offs3)
         nc.sync.dma_start(out=so_sb[:], in_=so.rearrange("(p t) j -> p t j", t=PACK))
         nc.sync.dma_start(out=fl_sb[:], in_=fl.rearrange("(p t) o -> p (t o)", t=PACK))
-        nc.sync.dma_start(out=xo_sb[1][:], in_=xo_rows[:, 1, :])
-        load_scale_rows(w2_scale_raw, w2_scales, range(0, 3))
-        nc.sync.dma_start(out=xo_sb[2][:], in_=xo_rows[:, 2, :])
-        load_scale_rows(w2_scale_raw, w2_scales, range(3, 4))
-        nc.sync.dma_start(out=xo_sb[3][:], in_=xo_rows[:, 3, :])
-        load_scale_rows(w_scale_raw, w_scales, range(0, 2))
+        nc.sync.dma_start(out=xo_planes[1], in_=xo_rows[:, Z : 2 * Z])
+        load_scale_rows(nc.sync, w2_scale_raw, w2_scales, range(0, 2))
+        nc.sync.dma_start(out=xo_planes[2], in_=xo_rows[:, 2 * Z : 3 * Z])
+        load_scale_rows(nc.sync, w2_scale_raw, w2_scales, range(2, 4))
+        nc.sync.dma_start(out=xo_planes[3], in_=xo_rows[:, 3 * Z : 4 * Z])
         nc.sync.dma_start(out=w2_raw[:].bitcast(I32), in_=w2_words[0].rearrange("p n t -> p (n t)").bitcast(I32))
+        nc.sync.dma_start(out=xa_first[:], in_=x_rows[0][:, 0 : 3 * T])
         nc.sync.dma_start(lists[0][:], offs)
-        nc.sync.dma_start(out=xa_pair[:], in_=x_rows[0][:, 0 : 2 * T])
-        load_scale_rows(w_scale_raw, w_scales, range(2, 4))
-        load_plane(0, 2)
         nc.sync.dma_start(out=w_raw[:].bitcast(I32), in_=w_words[0].bitcast(I32))
         load_plane(0, 3)
+        load_plane(1, 0)
         nc.sync.dma_start(lists[1][:], offs2)
-        for t in range(PACK):
+        for t in range(1, PACK):
             load_plane(1, t)
-        load_scale_rows(wb_scale, wb_scales, range(4))
         nc.sync.dma_start(out=wb_sb[:].bitcast(I32), in_=wb_words[0].rearrange("p n t -> p (n t)").bitcast(I32))
         nc.sync.dma_start(out=rs_sb[:], in_=rs.rearrange("(h p) n -> p h n", h=2))
 
@@ -93,7 +93,7 @@ def tile_list_sum_joined_largest_plain_rowpeaks_kernel(
         larger = [sb.tile([P, J], F32, name="larger%d" % t, align_bytes=64) for t in range(PACK)]
 
         def side_gather(t, j0, j1):
-            nc.scalar.activation(picked[t][:, j0:j1], xo_sb[t][:].indirect(list_o[:, j0 // 16 : j1 // 16]), ACT.Copy)
+            nc.scalar.activation(picked[t][:, j0:j1], xo_planes[t].indirect(list_o[:, j0 // 16 : j1 // 16]), ACT.Copy)
 
         def side_larger(t, j0, j1):
             nc.vector.tensor_tensor(larger[t][:, j0:j1], picked[t][:, j0:j1], so_sb[:, t, j0:j1], ALU.max)

@@ -54,9 +54,10 @@ def tile_list_sum_joined_largest_plain_rowpeaks_kernel(
         wb_sb = sb.tile([P, N], U32, align_bytes=64)
         xa_first = sb.tile([P, 3 * T], F32)
         xa_last = sb.tile([P, T], F32)
+        xb_first = sb.tile([P, 2 * S], F32)
         planes = [
             [xa_first[:, t * T : (t + 1) * T] for t in range(3)] + [xa_last[:]],
-            [sb.tile([P, S], F32, name="xb%d" % t)[:] for t in range(PACK)],
+            [xb_first[:, 0:S], xb_first[:, S : 2 * S]] + [sb.tile([P, S], F32, name="xb%d" % t)[:] for t in (2, 3)],
         ]
         rs_sb = sb.tile([P, 2, N], F32)
         x_rows = [xa.rearrange("(p t) c -> p (t c)", t=PACK), xb.rearrange("(p t) c -> p (t c)", t=PACK)]
@@ -78,9 +79,9 @@ def tile_list_sum_joined_largest_plain_rowpeaks_kernel(
         nc.sync.dma_start(lists[0][:], offs)
         nc.sync.dma_start(out=w_raw[:].bitcast(I32), in_=w_words[0].bitcast(I32))
         load_plane(0, 3)
-        load_plane(1, 0)
+        nc.sync.dma_start(out=xb_first[:], in_=x_rows[1][:, 0 : 2 * S])
         nc.sync.dma_start(lists[1][:], offs2)
-        for t in range(1, PACK):
+        for t in range(2, PACK):
             load_plane(1, t)
         nc.sync.dma_start(out=wb_sb[:].bitcast(I32), in_=wb_words[0].rearrange("p n t -> p (n t)").bitcast(I32))
         nc.sync.dma_start(out=rs_sb[:], in_=rs.rearrange("(h p) n -> p h n", h=2))
@@ -119,7 +120,7 @@ def tile_list_sum_joined_largest_plain_rowpeaks_kernel(
         hid_bf = []
         p_ps = [ps.tile([P, N], F32, name="p_ps%d" % h) for h in range(2)]
 
-        hid_ps = [ps.tile([P, PACK, HALF], F32, name="hid_ps%d" % h) for h in range(2)]
+        hid_ps = [[ps.tile([P, 2, HALF], F32, name="hid_ps%d_%d" % (h, b)) for b in range(2)] for h in range(2)]
 
         def gather_pair(h):
             pair = sb.tile([P, 2, HALF], F32, name="pair%d" % h, align_bytes=64)
@@ -140,13 +141,13 @@ def tile_list_sum_joined_largest_plain_rowpeaks_kernel(
         def first_layer_passes(h, weights, weight_scale, moving, opens):
             for t in range(PACK):
                 nc.tensor.matmul_mx(
-                    out=hid_ps[h][:, t, :],
+                    out=hid_ps[h][t // 2][:, t % 2, :],
                     lhsT=weights[t],
                     lhsT_scale=weight_scale[:, t * P : (t + 1) * P],
                     rhs=moving[0],
                     rhs_scale=moving[1],
-                    start=(opens and t == 0),
-                    stop=(not opens and t == PACK - 1),
+                    start=(opens and t % 2 == 0),
+                    stop=(not opens and t % 2 == 1),
                 )
 
         w_slices = [w_dealt[:, 2 * t * P : 2 * (t + 1) * P].bitcast(E2M1) for t in range(PACK)]
@@ -154,7 +155,10 @@ def tile_list_sum_joined_largest_plain_rowpeaks_kernel(
 
         def relu(h):
             hid_bf.append(sb.tile([P, HALF, PACK], BF16, name="hid_bf%d" % h, align_bytes=64))
-            nc.scalar.activation(hid_bf[h][:], hid_ps[h][:].rearrange("p t j -> p j t"), ACT.Relu)
+            for b in range(2):
+                nc.scalar.activation(
+                    hid_bf[h][:, :, 2 * b : 2 * b + 2], hid_ps[h][b][:].rearrange("p t j -> p j t"), ACT.Relu
+                )
 
         def second_layer(h):
             hid_codes = sb.tile([P, HALF], U32, name="hid_codes%d" % h, tag="u_bf1" if h == 0 else "hid_codes1", align_bytes=64)

from contextlib import ExitStack

import concourse.mybir as mybir

K, T, J, S, R, F, Z, N = 512, 512, 256, 512, 512, 512, 1024, 256
FLOPS = 2 * J * (K * R + F * R + R * N)

F32 = mybir.dt.float32
BF16 = mybir.dt.bfloat16
I32 = mybir.dt.int32
U32 = mybir.dt.uint32
U16 = mybir.dt.uint16
U8 = mybir.dt.uint8
E4M3 = mybir.dt.float8_e4m3fn_x4
E5M2 = mybir.dt.float8_e5m2_x4
E2M1 = mybir.dt.float4_e2m1fn_x4
ALU = mybir.AluOpType
ACT = mybir.ActivationFunctionType

P = 128
PACK = 4
HALF = 128


def tile_list_sum_joined_largest_plain_rowpeaks_kernel(
    tc, xa, xb, w_words, w_scales, xo, fl, so, w2_words, w2_scales, wb_words, wb_scales, rs, offs, offs2, offs3, out
):
    nc = tc.nc
    with ExitStack() as ctx:
        sb = ctx.enter_context(tc.tile_pool(name="sb", bufs=1))
        ps = ctx.enter_context(tc.psum_pool(name="ps", bufs=1))

        def load_scale_rows(queue, tile, scales, quadrants):
            rows = scales[0].bitcast(I32)
            for q in quadrants:
                queue.dma_start(out=tile[32 * q : 32 * q + 4, :].bitcast(I32), in_=rows[4 * q : 4 * q + 4, :])

        w2_scale_raw = sb.tile([P, R], U8)
        w_scale_raw = sb.tile([P, R], U8)
        wb_scale = sb.tile([P, N], U8, align_bytes=64)
        fl_sb = sb.tile([P, PACK], F32)
        nc.vector.memset(w2_scale_raw[:].bitcast(I32), 0)
        for tile, scales in ((w_scale_raw, w_scales), (wb_scale, wb_scales)):
            nc.gpsimd.memset(tile[:].bitcast(I32), 0)
            load_scale_rows(nc.gpsimd, tile, scales, range(4))

        xo_rows = xo.rearrange("(p t) z -> p (t z)", t=PACK)
        so_sb = sb.tile([P, PACK, J], F32)
        xo_planes = [sb.tile([P, Z], F32, name="xo%d" % t)[:] for t in range(PACK)]
        list_o = sb.tile([P, J // 16], U16)
        lists = [sb.tile([P, HALF // 16], U16, name="list_a"), sb.tile([P, HALF // 16], U16, name="list_b")]
        w2_raw = sb.tile([P, R], U32)
        w_raw = sb.tile([P, 2 * R], U8)
        wb_sb = sb.tile([P, N], U32, align_bytes=64)
        xa_first = sb.tile([P, 3 * T], F32)
        xa_last = sb.tile([P, T], F32)
        xb_first = sb.tile([P, 2 * S], F32)
        planes = [
            [xa_first[:, t * T : (t + 1) * T] for t in range(3)] + [xa_last[:]],
            [xb_first[:, 0:S], xb_first[:, S : 2 * S]] + [sb.tile([P, S], F32, name="xb%d" % t)[:] for t in (2, 3)],
        ]
        rs_sb = sb.tile([P, 2, N], F32)
        x_rows = [xa.rearrange("(p t) c -> p (t c)", t=PACK), xb.rearrange("(p t) c -> p (t c)", t=PACK)]

        def load_plane(h, t):
            nc.sync.dma_start(out=planes[h][t], in_=x_rows[h][:, t * T : (t + 1) * T])

        nc.sync.dma_start(out=xo_planes[0], in_=xo_rows[:, 0:Z])
        nc.sync.dma_start(list_o[:], offs3)
        nc.sync.dma_start(out=so_sb[:], in_=so.rearrange("(p t) j -> p t j", t=PACK))
        nc.sync.dma_start(out=fl_sb[:], in_=fl.rearrange("(p t) o -> p (t o)", t=PACK))
        nc.sync.dma_start(out=xo_planes[1], in_=xo_rows[:, Z : 2 * Z])
        load_scale_rows(nc.sync, w2_scale_raw, w2_scales, range(0, 2))
        nc.sync.dma_start(out=xo_planes[2], in_=xo_rows[:, 2 * Z : 3 * Z])
        load_scale_rows(nc.sync, w2_scale_raw, w2_scales, range(2, 4))
        nc.sync.dma_start(out=xo_planes[3], in_=xo_rows[:, 3 * Z : 4 * Z])
        nc.sync.dma_start(out=w2_raw[:].bitcast(I32), in_=w2_words[0].rearrange("p n t -> p (n t)").bitcast(I32))
        nc.sync.dma_start(out=xa_first[:], in_=x_rows[0][:, 0 : 3 * T])
        nc.sync.dma_start(lists[0][:], offs)
        nc.sync.dma_start(out=w_raw[:].bitcast(I32), in_=w_words[0].bitcast(I32))
        load_plane(0, 3)
        nc.sync.dma_start(out=xb_first[:], in_=x_rows[1][:, 0 : 2 * S])
        nc.sync.dma_start(lists[1][:], offs2)
        for t in range(2, PACK):
            load_plane(1, t)
        nc.sync.dma_start(out=wb_sb[:].bitcast(I32), in_=wb_words[0].rearrange("p n t -> p (n t)").bitcast(I32))
        nc.sync.dma_start(out=rs_sb[:], in_=rs.rearrange("(h p) n -> p h n", h=2))

        def deal_columns(copy, dealt, raw):
            copy(out=dealt.rearrange("p (t m) -> p m t", t=PACK), in_=raw.rearrange("p (m t) -> p m t", t=PACK))

        u2_bf = sb.tile([P, J, PACK], BF16, align_bytes=64)
        picked = [sb.tile([P, J], F32, name="picked%d" % t) for t in range(PACK)]
        larger = [sb.tile([P, J], F32, name="larger%d" % t, align_bytes=64) for t in range(PACK)]

        def side_gather(t, j0, j1):
            nc.scalar.activation(picked[t][:, j0:j1], xo_planes[t].indirect(list_o[:, j0 // 16 : j1 // 16]), ACT.Copy)

        def side_larger(t, j0, j1):
            nc.vector.tensor_tensor(larger[t][:, j0:j1], picked[t][:, j0:j1], so_sb[:, t, j0:j1], ALU.max)

        def side_scale(t, j0, j1):
            nc.vector.tensor_scalar(u2_bf[:, j0:j1, t], larger[t][:, j0:j1], fl_sb[:, t : t + 1], None, ALU.mult)

        for t in range(PACK - 1):
            side_gather(t, 0, J)
            side_larger(t, 0, J)
            if t == PACK - 2:
                w2_scale = sb.tile([P, R], U8, tag="larger1", align_bytes=64)
                deal_columns(nc.vector.tensor_copy, w2_scale[:], w2_scale_raw[:])
            side_scale(t, 0, J)
        for step in (side_gather, side_larger, side_scale):
            for h in range(2):
                step(PACK - 1, h * HALF, (h + 1) * HALF)
        w2_dealt = sb.tile([P, R], U32, align_bytes=64)
        deal_columns(nc.scalar.copy, w2_dealt[:], w2_raw[:])
        w_dealt = sb.tile([P, 2 * R], U8, align_bytes=64)

        u_bf = [sb.tile([P, HALF, PACK], BF16, name="u_bf%d" % h, align_bytes=64) for h in range(2)]
        hid_bf = []
        p_ps = [ps.tile([P, N], F32, name="p_ps%d" % h) for h in range(2)]

        hid_ps = [[ps.tile([P, 2, HALF], F32, name="hid_ps%d_%d" % (h, b)) for b in range(2)] for h in range(2)]

        def gather_pair(h):
            pair = sb.tile([P, 2, HALF], F32, name="pair%d" % h, align_bytes=64)
            for t in range(2):
                nc.scalar.activation(pair[:, t, :], planes[h][t].indirect(lists[h][:]), ACT.Copy)
            gather(h, 2)
            nc.vector.tensor_copy(u_bf[h][:, :, 0:2], pair[:].rearrange("p t j -> p j t"))

        def gather(h, t):
            nc.vector.tensor_copy(u_bf[h][:, :, t], planes[h][t].indirect(lists[h][:]))

        def quantise(values, fmt, name, tag):
            codes = sb.tile([P, HALF], U32, name=name + "_codes", tag=tag, align_bytes=64)
            scale = sb.tile([P, HALF], U8, name=name + "_scale", align_bytes=64)
            nc.vector.quantize_mx(out=codes[:].bitcast(fmt), scales=scale[:], in_=values.rearrange("p j t -> p (j t)"))
            return codes[:].bitcast(fmt), scale[:]

        def first_layer_passes(h, weights, weight_scale, moving, opens):
            for t in range(PACK):
                nc.tensor.matmul_mx(
                    out=hid_ps[h][t // 2][:, t % 2, :],
                    lhsT=weights[t],
                    lhsT_scale=weight_scale[:, t * P : (t + 1) * P],
                    rhs=moving[0],
                    rhs_scale=moving[1],
                    start=(opens and t % 2 == 0),
                    stop=(not opens and t % 2 == 1),
                )

        w_slices = [w_dealt[:, 2 * t * P : 2 * (t + 1) * P].bitcast(E2M1) for t in range(PACK)]
        w2_slices = [w2_dealt[:, t * P : (t + 1) * P].bitcast(E5M2) for t in range(PACK)]

        def relu(h):
            hid_bf.append(sb.tile([P, HALF, PACK], BF16, name="hid_bf%d" % h, align_bytes=64))
            for b in range(2):
                nc.scalar.activation(
                    hid_bf[h][:, :, 2 * b : 2 * b + 2], hid_ps[h][b][:].rearrange("p t j -> p j t"), ACT.Relu
                )

        def second_layer(h):
            hid_codes = sb.tile([P, HALF], U32, name="hid_codes%d" % h, tag="u_bf1" if h == 0 else "hid_codes1", align_bytes=64)
            hid_scale = sb.tile([P, HALF], U8, name="hid_scale%d" % h, align_bytes=64)
            nc.vector.quantize_mx(
                out=hid_codes[:].bitcast(E5M2), scales=hid_scale[:], in_=hid_bf[h][:].rearrange("p j t -> p (j t)")
            )
            nc.tensor.matmul_mx(
                out=p_ps[h][:],
                lhsT=hid_codes[:].bitcast(E5M2),
                lhsT_scale=hid_scale[:],
                rhs=wb_sb[:].bitcast(E5M2),
                rhs_scale=wb_scale[:],
                start=True,
                stop=True,
            )

        inverse = [sb.tile([P, 1], F32, name="inverse%d" % h) for h in range(2)]
        residual = sb.tile([P, 2, N], F32)

        def row_peaks(h):
            size = sb.tile([P, N], F32, name="size%d" % h)
            divisor = sb.tile([P, 1], F32, name="divisor%d" % h)
            nc.scalar.activation(size[:], p_ps[h][:], ACT.Abs)
            nc.vector.tensor_scalar(size[:], size[:], 0.2, None, ALU.add, ALU.max, accum_out=divisor[:])
            nc.vector.reciprocal(inverse[h][:], divisor[:])

        def finish(h):
            result = sb.tile([P, N], F32, name="result%d" % h)
            nc.vector.scalar_tensor_tensor(result[:], p_ps[h][:], inverse[h][:], residual[:, h, :], ALU.mult, ALU.add)
            nc.sync.dma_start(out=out[h * HALF : (h + 1) * HALF, :], in_=result[:])

        w_scale = sb.tile([P, R], U8, tag="larger3", align_bytes=64)
        deal_columns(nc.vector.tensor_copy, w_scale[:], w_scale_raw[:])
        gather_pair(0)
        deal_columns(nc.scalar.copy, w_dealt[:].bitcast(U16), w_raw[:].bitcast(U16))
        u2_first = quantise(u2_bf[:, 0:HALF, :], E5M2, "u2_first", "u2_first_codes")
        first_layer_passes(0, w2_slices, w2_scale, u2_first, True)
        gather(0, 3)
        u_first = quantise(u_bf[0][:], E4M3, "u_first", "u_first_codes")
        first_layer_passes(0, w_slices, w_scale, u_first, False)
        u2_second = quantise(u2_bf[:, HALF:J, :], E5M2, "u2_second", "u2_second_codes")
        first_layer_passes(1, w2_slices, w2_scale, u2_second, True)
        for t in range(PACK):
            gather(1, t)
        relu(0)
        u_second = quantise(u_bf[1][:], E4M3, "u_second", "u_second_codes")
        first_layer_passes(1, w_slices, w_scale, u_second, False)
        relu(1)
        second_layer(0)
        nc.vector.tensor_scalar(residual[:], rs_sb[:], 0.3, None, ALU.mult)
        second_layer(1)
        row_peaks(0)
        finish(0)
        row_peaks(1)
        finish(1)
